import numpy as np
import ml_dtypes


def mxq(x, axis, fmt="e4m3"):
    dtype, down = {"e4m3": (ml_dtypes.float8_e4m3fn, 7), "e5m2": (ml_dtypes.float8_e5m2, 14)}[fmt]
    v = np.moveaxis(np.asarray(x, np.float32).astype(ml_dtypes.bfloat16).astype(np.float64), axis, -1)
    blocks = v.reshape(v.shape[:-1] + (-1, 32))
    amax = np.abs(blocks).max(-1, keepdims=True)
    byte = np.maximum(np.where(amax > 0, np.frexp(amax)[1] - 1 + 127, 0) - down, 1)
    scale = np.exp2(byte - 127.0)
    codes = (blocks / scale).astype(np.float32).astype(dtype).astype(np.float64)
    return np.moveaxis((codes * scale).reshape(v.shape), -1, axis)


WIDE = False


def mx_kscale(k):
    if not WIDE:
        return np.ones(k)
    levels = np.array([10, -10, 5, -5, 0])
    if k % 512:
        return np.exp2(np.random.permutation(np.resize(levels, k // 32))).repeat(32)
    a = np.empty((k // 512, 16))
    for p in range(k // 512):
        a[p, :8] = np.random.permutation(np.resize(levels, 8))
        for g in range(8):
            far = levels[np.abs(levels - a[p, g]) >= 10]
            a[p, g + 8] = far[np.random.randint(len(far))]
    return np.exp2(a.ravel()).repeat(32)


BF16 = ml_dtypes.bfloat16


def bf(x):
    return np.asarray(x, np.float32).astype(BF16)


def f64(x):
    return np.asarray(x).astype(np.float64)


E2M1 = np.array([0.0, 0.5, 1.0, 1.5, 2.0, 3.0, 4.0, 6.0, -0.0, -0.5, -1.0, -1.5, -2.0, -3.0, -4.0, -6.0])


def pack_weight(w, fmt):
    k, n = w.shape
    w = f64(bf(w)).reshape(k // 32, 32, n)
    amax = np.abs(w).max(1)
    if fmt == "e4m3":
        byte = np.frexp(amax)[1] - 1 + 127 - 7
    else:
        mant, ex = np.frexp(amax / 6.0)
        byte = np.where(mant > 0.5, ex, ex - 1) + 127
    byte = np.clip(np.where(amax > 0, byte, 1), 1, 254)
    scaled = (w * np.exp2(127.0 - byte)[:, None, :]).reshape(k, n).astype(np.float32)
    by_word = np.ascontiguousarray(scaled.reshape(k // 512, 128, 4, n).transpose(0, 1, 3, 2))
    if fmt == "e4m3":
        words = by_word.astype(ml_dtypes.float8_e4m3fn).view(np.uint8)
    else:
        c = by_word.astype(ml_dtypes.float4_e2m1fn).view(np.uint8) & 0xF
        words = c[..., 0::2] | (c[..., 1::2] << 4)
    return np.ascontiguousarray(words), np.ascontiguousarray(byte.astype(np.uint8).reshape(k // 512, 16, n))


def unpack_weight(words, scales, fmt):
    g, p, n, _ = words.shape
    if fmt == "e4m3":
        vals = np.ascontiguousarray(words).view(ml_dtypes.float8_e4m3fn).astype(np.float64)
    else:
        nib = np.empty((g, p, n, 4), np.uint8)
        nib[..., 0::2] = words & 0xF
        nib[..., 1::2] = words >> 4
        vals = E2M1[nib]
    vals = vals * np.repeat(np.exp2(scales.astype(np.float64) - 127.0), 8, axis=1)[..., None]
    return vals.transpose(0, 1, 3, 2).reshape(g * 512, n)
def pack4(w):
    words, scales = pack_weight(w, "e2m1")
    return words.reshape(words.shape[0], 128, -1), scales


def unpack4(words, scales):
    return unpack_weight(words.reshape(words.shape[0], 128, -1, 2), scales, "e2m1")


def planes(Y):
    n, m = Y.shape
    b = f64(bf(Y)).reshape(n // 32, 32, m)
    amax = np.abs(b).max(1)
    byte = np.clip(np.where(amax > 0, np.frexp(amax)[1] - 1 + 127 - 7, 1), 1, 254)
    codes = (b * np.exp2(127.0 - byte)[:, None, :]).reshape(n, m).astype(np.float32).astype(ml_dtypes.float8_e4m3fn).view(np.uint8)
    words = codes.reshape(n // 512, 128, 4, m).transpose(0, 1, 3, 2)
    return np.ascontiguousarray(words), np.ascontiguousarray(byte.astype(np.uint8).reshape(n // 512, 16, m))


M, C = 1024, 2048


def setup_inputs():
    s = mx_kscale(C)
    x = np.random.randn(M, C)
    x_words, x_scales = pack_weight((x * s).T, "e4m3")
    w_r = np.random.randn(C, C) * 2.0 / np.sqrt(C)
    den_state = bf(np.exp(0.5 * np.random.randn(M, C)))
    spread = np.exp(0.8 * np.random.randn(C))
    value = np.random.randn(M, C) * spread
    num_state = bf(value * f64(den_state))
    return {
        "x_words": x_words,
        "x_scales": x_scales,
        "w_r": bf(w_r / s[:, None]),
        "num_state": num_state,
        "den_state": den_state,
    }

def reference(x_words, x_scales, w_r, num_state, den_state):
    xt = unpack_weight(x_words, x_scales, "e4m3")
    z = xt.T @ mxq(f64(w_r), 0, "e4m3")
    r = 1.0 / (1.0 + np.exp(-z))
    y = r * (f64(num_state) / f64(den_state))
    words, scales = planes(y.T)
    return y, words, scales

@@ -1,0 +1,263 @@
+from contextlib import ExitStack
+
+import concourse.mybir as mybir
+from concourse.masks import make_identity
+
+M, C = 1024, 2048
+FLOPS = 2 * M * C * C
+
+F32 = mybir.dt.float32
+BF16 = mybir.dt.bfloat16
+I32 = mybir.dt.int32
+U32 = mybir.dt.uint32
+U8 = mybir.dt.uint8
+FP8X4 = mybir.dt.float8_e4m3fn_x4
+ACT = mybir.ActivationFunctionType
+MULT = mybir.AluOpType.mult
+
+P = 128
+PACK = 4
+K_PASS = P * PACK
+PASSES = C // K_PASS
+BANK = 512
+HALF = 1024
+ROW_TILES = M // P
+STEPS = 2 * ROW_TILES
+X_PART = 512
+PLANE_TOK = 512
+
+
+def tile_receptance_gated_state_readout_g6_kernel(
+    tc, x_words, x_scales, w_r, num_state, den_state, out_0, out_1, out_2
+):
+    nc = tc.nc
+    with ExitStack() as ctx:
+        keep = ctx.enter_context(tc.tile_pool(name="keep", bufs=1))
+        stream = ctx.enter_context(tc.tile_pool(name="stream", bufs=3))
+        psum = ctx.enter_context(tc.psum_pool(name="psum", bufs=2))
+        ctx.enter_context(tc.manual_schedule())
+
+        x_plane = keep.tile([P, M], U8, align_bytes=64)
+        nc.gpsimd.memset(x_plane[:].bitcast(I32), 0)
+        ident = keep.tile([P, P], F32)
+        make_identity(nc, ident[:])
+
+        w_raw, w_grouped, w_codes, w_planes = {}, {}, {}, {}
+        x_codes, state, work, z, gate = {}, {}, {}, {}, {}
+        y_bf, turned, y_grouped, y_codes, y_planes = {}, {}, {}, {}, {}
+
+        def load_w(slab, blocks):
+            half, g = divmod(slab, PASSES)
+            lo, hi = blocks[0] * BANK, (blocks[-1] + 1) * BANK
+            raw = stream.tile([P, PACK, hi - lo], BF16, name="w_raw", bufs=3)
+            rows = w_r[g * K_PASS : (g + 1) * K_PASS, half * HALF + lo : half * HALF + hi]
+            nc.sync.dma_start(out=raw[:], in_=rows.rearrange("(p j) n -> p j n", j=PACK))
+            for block in blocks:
+                w_raw[2 * slab + block] = raw[:, :, block * BANK - lo : (block + 1) * BANK - lo]
+
+        def interleave_w(unit):
+            w_grouped[unit] = stream.tile([P, BANK * PACK], BF16, name="w_grouped", bufs=3, align_bytes=64)
+            nc.vector.tensor_copy(
+                out=w_grouped[unit][:].rearrange("p (c i j) -> p c j i", i=4, j=PACK),
+                in_=w_raw[unit].rearrange("p j (c i) -> p c j i", i=4),
+            )
+
+        def quantize_w(unit):
+            w_codes[unit] = keep.tile([P, BANK], U32, name="w_codes%d" % unit, align_bytes=64)
+            w_planes[unit] = keep.tile([P, BANK], U8, name="w_plane%d" % unit, align_bytes=64)
+            nc.vector.quantize_mx(
+                out=w_codes[unit][:].bitcast(FP8X4), scales=w_planes[unit][:], in_=w_grouped[unit][:]
+            )
+
+        def load_state(src, key, m):
+            state[key, m] = stream.tile([P, C], BF16, name="state", bufs=ROW_TILES)
+            nc.sync.dma_start(out=state[key, m][:], in_=src[m * P : (m + 1) * P, :])
+
+        def load_x_scales():
+            for quad in range(4):
+                nc.sync.dma_start(
+                    out=x_plane[32 * quad : 32 * quad + 16, :].bitcast(I32),
+                    in_=x_scales[:, 4 * quad : 4 * quad + 4, :].bitcast(I32),
+                )
+
+        def load_x(part):
+            x_codes[part] = keep.tile([P, PASSES, X_PART], U32, name="x_codes%d" % part, align_bytes=64)
+            merged = x_words.rearrange("g p n t -> p g (n t)")
+            lo = part * X_PART * PACK
+            nc.sync.dma_start(
+                out=x_codes[part][:].bitcast(I32), in_=merged[:, :, lo : lo + X_PART * PACK].bitcast(I32)
+            )
+
+        def inverse_root(m):
+            work[m] = keep.tile([P, C], F32, name="work%d" % m)
+            nc.scalar.activation(out=work[m][:], in_=state["den", m][:], func=ACT.Abs_reciprocal_sqrt)
+
+        def work_of(step):
+            half, m = divmod(step, ROW_TILES)
+            return work[m][:, half * HALF : (half + 1) * HALF]
+
+        def square(step):
+            nc.scalar.activation(out=work_of(step), in_=work_of(step), func=ACT.Square)
+
+        def square_on_vector(step):
+            nc.vector.tensor_tensor(out=work_of(step), in0=work_of(step), in1=work_of(step), op=MULT)
+
+        def readout(step):
+            half, m = divmod(step, ROW_TILES)
+            num = state["num", m][:, half * HALF : (half + 1) * HALF]
+            nc.vector.tensor_tensor(out=work_of(step), in0=work_of(step), in1=num, op=MULT)
+
+        def project(step):
+            half, m = divmod(step, ROW_TILES)
+            part, lo = divmod(m * P, X_PART)
+            for block in range(2):
+                z[step, block] = psum.tile([P, BANK], F32, name="z", bufs=6)
+                for g in range(PASSES):
+                    unit = 2 * (half * PASSES + g) + block
+                    nc.tensor.matmul_mx(
+                        out=z[step, block][:],
+                        lhsT=x_codes[part][:, g, lo : lo + P].bitcast(FP8X4),
+                        lhsT_scale=x_plane[4 * g :, m * P : (m + 1) * P],
+                        rhs=w_codes[unit][:].bitcast(FP8X4),
+                        rhs_scale=w_planes[unit][:],
+                        start=(g == 0),
+                        stop=(g == PASSES - 1),
+                    )
+
+        def receptance(step):
+            gate[step] = stream.tile([P, HALF], F32, name="gate", bufs=3)
+            for block in range(2):
+                nc.scalar.activation(
+                    out=gate[step][:, block * BANK : (block + 1) * BANK], in_=z[step, block][:], func=ACT.Sigmoid
+                )
+
+        def apply_gate(step):
+            nc.vector.tensor_tensor(out=work_of(step), in0=work_of(step), in1=gate[step][:], op=MULT)
+
+        def round_y(step, copy):
+            y_bf[step] = stream.tile([P, HALF], BF16, name="y_bf", bufs=2)
+            copy(
+                out=y_bf[step][:].rearrange("p (u w e) -> p u w e", u=2, e=2),
+                in_=work_of(step).rearrange("p (w u e) -> p u w e", u=2, e=2),
+            )
+
+        def turn(step):
+            turned[step] = psum.tile([P, 2, 2, P], F32, name="turned", bufs=2)
+            words = y_bf[step][:].bitcast(F32)
+            for block in range(2):
+                for u in range(2):
+                    lo = (2 * u + block) * P
+                    nc.tensor.transpose(turned[step][:, block, u, :], words[:, lo : lo + P], ident[:])
+
+        def gather_words(step):
+            y_grouped[step] = stream.tile([P, HALF], BF16, name="y_grouped", bufs=3, align_bytes=64)
+            nc.scalar.copy(
+                out=y_grouped[step][:].bitcast(F32).rearrange("p (b m u) -> p b m u", b=2, u=2),
+                in_=turned[step][:].rearrange("p b u m -> p b m u"),
+            )
+
+        def quantize_y(step):
+            half, m = divmod(step, ROW_TILES)
+            piece, lo = divmod(m * P, PLANE_TOK)
+            if m == 0:
+                y_planes[half] = keep.tile([P, 2, M], U8, name="y_plane%d" % half, align_bytes=64)
+            for block in range(2):
+                g = 2 * half + block
+                if lo == 0:
+                    y_codes[g, piece] = keep.tile(
+                        [P, PLANE_TOK], U32, name="y_codes%d_%d" % (g, piece), align_bytes=64
+                    )
+                nc.vector.quantize_mx(
+                    out=y_codes[g, piece][:, lo : lo + P].bitcast(FP8X4),
+                    scales=y_planes[half][:, block, m * P : (m + 1) * P],
+                    in_=y_grouped[step][:, block * BANK : (block + 1) * BANK],
+                )
+
+        def store_y(step):
+            half, m = divmod(step, ROW_TILES)
+            nc.sync.dma_start(out=out_0[m * P : (m + 1) * P, half * HALF : (half + 1) * HALF], in_=work_of(step))
+
+        def store_planes(step):
+            half, m = divmod(step, ROW_TILES)
+            piece, lo = divmod(m * P, PLANE_TOK)
+            if lo + P == PLANE_TOK:
+                for block in range(2):
+                    g = 2 * half + block
+                    merged = out_1[g].rearrange("p m t -> p (m t)")
+                    b0 = piece * PLANE_TOK * PACK
+                    nc.sync.dma_start(
+                        out=merged[:, b0 : b0 + PLANE_TOK * PACK].bitcast(I32), in_=y_codes[g, piece][:].bitcast(I32)
+                    )
+            if m == ROW_TILES - 1:
+                for quad in range(4):
+                    rows = out_2[2 * half : 2 * half + 2, 4 * quad : 4 * quad + 4, :]
+                    nc.sync.dma_start(
+                        out=rows.rearrange("g r m -> r g m").bitcast(I32),
+                        in_=y_planes[half][32 * quad : 32 * quad + 4, :, :].bitcast(I32),
+                    )
+
+        def prepare_w(slab):
+            for unit in (2 * slab, 2 * slab + 1):
+                interleave_w(unit)
+                if unit > 0:
+                    quantize_w(unit - 1)
+
+        X_AFTER = 4
+        for m in range(ROW_TILES):
+            if m == 0:
+                load_w(0, [0])
+                load_state(den_state, "den", 0)
+                load_w(0, [1])
+            elif m <= X_AFTER:
+                load_w(m, [0, 1])
+                load_state(den_state, "den", m)
+            else:
+                load_state(den_state, "den", m)
+                if m == ROW_TILES - 1:
+                    load_state(num_state, "num", 0)
+                load_w(m, [0, 1])
+            if m == X_AFTER:
+                load_x_scales()
+                load_x(0)
+            inverse_root(m)
+            if m < ROW_TILES - 1:
+                square(m)
+            if m == X_AFTER + 1:
+                square_on_vector(ROW_TILES)
+            if m == ROW_TILES - 1:
+                readout(0)
+            prepare_w(m)
+        load_state(num_state, "num", 1)
+        load_state(num_state, "num", 2)
+        load_x(1)
+        for m in range(3, ROW_TILES):
+            load_state(num_state, "num", m)
+        for step in range(3):
+            project(step)
+
+        to_square = [ROW_TILES - 1] + list(range(ROW_TILES + 1, STEPS))
+        for i in range(STEPS + 4):
+            if i < STEPS:
+                receptance(i)
+            if i % 2 == 0 and 2 <= i < STEPS:
+                round_y(i - 1, nc.scalar.copy)
+            elif to_square:
+                square(to_square.pop(0))
+            if 3 <= i < STEPS + 3:
+                gather_words(i - 3)
+            if i < STEPS:
+                apply_gate(i)
+                store_y(i)
+            if i == 0:
+                quantize_w(2 * ROW_TILES - 1)
+            if i + 1 < STEPS:
+                readout(i + 1)
+            if 4 <= i:
+                quantize_y(i - 4)
+                store_planes(i - 4)
+            if i < STEPS and (i % 2 == 0 or i == STEPS - 1):
+                round_y(i, nc.vector.tensor_copy)
+            if i + 3 < STEPS:
+                project(i + 3)
+            if 1 <= i < STEPS + 1:
+                turn(i - 1)

@@ -23,8 +23,12 @@ BANK = 512
 HALF = 1024
 ROW_TILES = M // P
 STEPS = 2 * ROW_TILES
-X_PART = 512
-PLANE_TOK = 512
+UNITS = C // BANK
+W_PIECES = [[(0, 1), (1, 2), (2, 4)], [(0, 2), (2, 4)], [(0, 4)], [(0, 4)]]
+X_PARTS = [(0, 2), (2, ROW_TILES)]
+WORD_PIECES = [(0, 2), (2, 4), (4, 6), (6, 7), (7, 8)]
+SCALE_PIECES = [(0, 7), (7, 8)]
+AHEAD = 3
 
 
 def tile_receptance_gated_state_readout_g6_kernel(
@@ -42,18 +46,19 @@ def tile_receptance_gated_state_readout_g6_kernel(
         ident = keep.tile([P, P], F32)
         make_identity(nc, ident[:])
 
-        w_raw, w_grouped, w_codes, w_planes = {}, {}, {}, {}
+        w_rows, w_raw, w_grouped, w_codes, w_planes = {}, {}, {}, {}, {}
         x_codes, state, work, z, gate = {}, {}, {}, {}, {}
         y_bf, turned, y_grouped, y_codes, y_planes = {}, {}, {}, {}, {}
 
-        def load_w(slab, blocks):
-            half, g = divmod(slab, PASSES)
-            lo, hi = blocks[0] * BANK, (blocks[-1] + 1) * BANK
-            raw = stream.tile([P, PACK, hi - lo], BF16, name="w_raw", bufs=3)
-            rows = w_r[g * K_PASS : (g + 1) * K_PASS, half * HALF + lo : half * HALF + hi]
-            nc.sync.dma_start(out=raw[:], in_=rows.rearrange("(p j) n -> p j n", j=PACK))
-            for block in blocks:
-                w_raw[2 * slab + block] = raw[:, :, block * BANK - lo : (block + 1) * BANK - lo]
+        def load_w(g, piece):
+            if g not in w_rows:
+                w_rows[g] = stream.tile([P, PACK * C], BF16, name="w_rows", bufs=2)
+            lo, hi = piece[0] * BANK, piece[1] * BANK
+            raw = w_rows[g][:, PACK * lo : PACK * hi].rearrange("p (j n) -> p j n", j=PACK)
+            rows = w_r[g * K_PASS : (g + 1) * K_PASS, lo:hi]
+            nc.sync.dma_start(out=raw, in_=rows.rearrange("(p j) n -> p j n", j=PACK))
+            for block in range(piece[0], piece[1]):
+                w_raw[UNITS * g + block] = raw[:, :, block * BANK - lo : (block + 1) * BANK - lo]
 
         def interleave_w(unit):
             w_grouped[unit] = stream.tile([P, BANK * PACK], BF16, name="w_grouped", bufs=3, align_bytes=64)
@@ -69,9 +74,10 @@ def tile_receptance_gated_state_readout_g6_kernel(
                 out=w_codes[unit][:].bitcast(FP8X4), scales=w_planes[unit][:], in_=w_grouped[unit][:]
             )
 
-        def load_state(src, key, m):
-            state[key, m] = stream.tile([P, C], BF16, name="state", bufs=ROW_TILES)
-            nc.sync.dma_start(out=state[key, m][:], in_=src[m * P : (m + 1) * P, :])
+        def load_state(src, key, m, lo=0, hi=C):
+            if (key, m) not in state:
+                state[key, m] = stream.tile([P, C], BF16, name="state", bufs=ROW_TILES)
+            nc.sync.dma_start(out=state[key, m][:, lo:hi], in_=src[m * P : (m + 1) * P, lo:hi])
 
         def load_x_scales():
             for quad in range(4):
@@ -81,19 +87,22 @@ def tile_receptance_gated_state_readout_g6_kernel(
                 )
 
         def load_x(part):
-            x_codes[part] = keep.tile([P, PASSES, X_PART], U32, name="x_codes%d" % part, align_bytes=64)
+            first, last = part
+            codes = keep.tile([P, PASSES, (last - first) * P], U32, name="x_codes%d" % first, align_bytes=64)
             merged = x_words.rearrange("g p n t -> p g (n t)")
-            lo = part * X_PART * PACK
             nc.sync.dma_start(
-                out=x_codes[part][:].bitcast(I32), in_=merged[:, :, lo : lo + X_PART * PACK].bitcast(I32)
+                out=codes[:].bitcast(I32), in_=merged[:, :, first * P * PACK : last * P * PACK].bitcast(I32)
             )
+            for m in range(first, last):
+                x_codes[m] = codes[:, :, (m - first) * P : (m - first + 1) * P]
 
-        def inverse_root(m):
-            work[m] = keep.tile([P, C], F32, name="work%d" % m)
-            nc.scalar.activation(out=work[m][:], in_=state["den", m][:], func=ACT.Abs_reciprocal_sqrt)
+        def inverse_root(m, lo=0, hi=C):
+            if m not in work:
+                work[m] = keep.tile([P, C], F32, name="work%d" % m)
+            nc.scalar.activation(out=work[m][:, lo:hi], in_=state["den", m][:, lo:hi], func=ACT.Abs_reciprocal_sqrt)
 
         def work_of(step):
-            half, m = divmod(step, ROW_TILES)
+            m, half = divmod(step, 2)
             return work[m][:, half * HALF : (half + 1) * HALF]
 
         def square(step):
@@ -103,26 +112,24 @@ def tile_receptance_gated_state_readout_g6_kernel(
             nc.vector.tensor_tensor(out=work_of(step), in0=work_of(step), in1=work_of(step), op=MULT)
 
         def readout(step):
-            half, m = divmod(step, ROW_TILES)
+            m, half = divmod(step, 2)
             num = state["num", m][:, half * HALF : (half + 1) * HALF]
             nc.vector.tensor_tensor(out=work_of(step), in0=work_of(step), in1=num, op=MULT)
 
-        def project(step):
-            half, m = divmod(step, ROW_TILES)
-            part, lo = divmod(m * P, X_PART)
-            for block in range(2):
-                z[step, block] = psum.tile([P, BANK], F32, name="z", bufs=6)
-                for g in range(PASSES):
-                    unit = 2 * (half * PASSES + g) + block
-                    nc.tensor.matmul_mx(
-                        out=z[step, block][:],
-                        lhsT=x_codes[part][:, g, lo : lo + P].bitcast(FP8X4),
-                        lhsT_scale=x_plane[4 * g :, m * P : (m + 1) * P],
-                        rhs=w_codes[unit][:].bitcast(FP8X4),
-                        rhs_scale=w_planes[unit][:],
-                        start=(g == 0),
-                        stop=(g == PASSES - 1),
-                    )
+        def project(step, block, g):
+            m, half = divmod(step, 2)
+            if g == 0:
+                z[step, block] = psum.tile([P, BANK], F32, name="z", bufs=2 * AHEAD)
+            unit = UNITS * g + 2 * half + block
+            nc.tensor.matmul_mx(
+                out=z[step, block][:],
+                lhsT=x_codes[m][:, g, :].bitcast(FP8X4),
+                lhsT_scale=x_plane[4 * g :, m * P : (m + 1) * P],
+                rhs=w_codes[unit][:].bitcast(FP8X4),
+                rhs_scale=w_planes[unit][:],
+                start=(g == 0),
+                stop=(g == PASSES - 1),
+            )
 
         def receptance(step):
             gate[step] = stream.tile([P, HALF], F32, name="gate", bufs=3)
@@ -137,8 +144,8 @@ def tile_receptance_gated_state_readout_g6_kernel(
         def round_y(step, copy):
             y_bf[step] = stream.tile([P, HALF], BF16, name="y_bf", bufs=2)
             copy(
-                out=y_bf[step][:].rearrange("p (u w e) -> p u w e", u=2, e=2),
-                in_=work_of(step).rearrange("p (w u e) -> p u w e", u=2, e=2),
+                out=y_bf[step][:].rearrange("p (b u w e) -> p b u w e", b=2, u=2, e=2),
+                in_=work_of(step).rearrange("p (b w u e) -> p b u w e", b=2, u=2, e=2),
             )
 
         def turn(step):
@@ -146,118 +153,143 @@ def tile_receptance_gated_state_readout_g6_kernel(
             words = y_bf[step][:].bitcast(F32)
             for block in range(2):
                 for u in range(2):
-                    lo = (2 * u + block) * P
+                    lo = (2 * block + u) * P
                     nc.tensor.transpose(turned[step][:, block, u, :], words[:, lo : lo + P], ident[:])
 
         def gather_words(step):
-            y_grouped[step] = stream.tile([P, HALF], BF16, name="y_grouped", bufs=3, align_bytes=64)
+            y_grouped[step] = stream.tile([P, HALF], BF16, name="y_grouped", bufs=2, align_bytes=64)
             nc.scalar.copy(
                 out=y_grouped[step][:].bitcast(F32).rearrange("p (b m u) -> p b m u", b=2, u=2),
                 in_=turned[step][:].rearrange("p b u m -> p b m u"),
             )
 
+        def piece_of(pieces, m):
+            return [piece for piece in pieces if piece[0] <= m < piece[1]][0]
+
         def quantize_y(step):
-            half, m = divmod(step, ROW_TILES)
-            piece, lo = divmod(m * P, PLANE_TOK)
-            if m == 0:
-                y_planes[half] = keep.tile([P, 2, M], U8, name="y_plane%d" % half, align_bytes=64)
+            m, half = divmod(step, 2)
+            words, scales = piece_of(WORD_PIECES, m), piece_of(SCALE_PIECES, m)
+            if words not in y_codes:
+                shape = [P, PASSES, (words[1] - words[0]) * P]
+                y_codes[words] = stream.tile(shape, U32, name="y_codes", bufs=3, align_bytes=64)
+            if scales not in y_planes:
+                shape = [P, PASSES, (scales[1] - scales[0]) * P]
+                y_planes[scales] = keep.tile(shape, U8, name="y_plane%d" % scales[0], align_bytes=64)
             for block in range(2):
                 g = 2 * half + block
-                if lo == 0:
-                    y_codes[g, piece] = keep.tile(
-                        [P, PLANE_TOK], U32, name="y_codes%d_%d" % (g, piece), align_bytes=64
-                    )
+                lo, lo_s = (m - words[0]) * P, (m - scales[0]) * P
                 nc.vector.quantize_mx(
-                    out=y_codes[g, piece][:, lo : lo + P].bitcast(FP8X4),
-                    scales=y_planes[half][:, block, m * P : (m + 1) * P],
+                    out=y_codes[words][:, g, lo : lo + P].bitcast(FP8X4),
+                    scales=y_planes[scales][:, g, lo_s : lo_s + P],
                     in_=y_grouped[step][:, block * BANK : (block + 1) * BANK],
                 )
 
-        def store_y(step):
-            half, m = divmod(step, ROW_TILES)
-            nc.sync.dma_start(out=out_0[m * P : (m + 1) * P, half * HALF : (half + 1) * HALF], in_=work_of(step))
+        def store_y(first, last):
+            m, half = divmod(first, 2)
+            lo, hi = half * HALF, (half + last - first) * HALF
+            nc.sync.dma_start(out=out_0[m * P : (m + 1) * P, lo:hi], in_=work[m][:, lo:hi])
 
         def store_planes(step):
-            half, m = divmod(step, ROW_TILES)
-            piece, lo = divmod(m * P, PLANE_TOK)
-            if lo + P == PLANE_TOK:
-                for block in range(2):
-                    g = 2 * half + block
-                    merged = out_1[g].rearrange("p m t -> p (m t)")
-                    b0 = piece * PLANE_TOK * PACK
-                    nc.sync.dma_start(
-                        out=merged[:, b0 : b0 + PLANE_TOK * PACK].bitcast(I32), in_=y_codes[g, piece][:].bitcast(I32)
-                    )
-            if m == ROW_TILES - 1:
+            m, half = divmod(step, 2)
+            words, scales = piece_of(WORD_PIECES, m), piece_of(SCALE_PIECES, m)
+            if half == 1 and m + 1 == words[1]:
+                merged = out_1.rearrange("g p m t -> p g (m t)")
+                nc.sync.dma_start(
+                    out=merged[:, :, words[0] * P * PACK : words[1] * P * PACK].bitcast(I32),
+                    in_=y_codes[words][:].bitcast(I32),
+                )
+            if half == 1 and m + 1 == scales[1]:
                 for quad in range(4):
-                    rows = out_2[2 * half : 2 * half + 2, 4 * quad : 4 * quad + 4, :]
-                    nc.sync.dma_start(
+                    rows = out_2[:, 4 * quad : 4 * quad + 4, scales[0] * P : scales[1] * P]
+                    queue = nc.scalar if step == STEPS - 1 and quad >= 2 else nc.sync
+                    queue.dma_start(
                         out=rows.rearrange("g r m -> r g m").bitcast(I32),
-                        in_=y_planes[half][32 * quad : 32 * quad + 4, :, :].bitcast(I32),
+                        in_=y_planes[scales][32 * quad : 32 * quad + 4, :, :].bitcast(I32),
                     )
 
-        def prepare_w(slab):
-            for unit in (2 * slab, 2 * slab + 1):
+        def prepare_w(first, last):
+            for unit in range(first, last):
                 interleave_w(unit)
-                if unit > 0:
+                if unit > first:
                     quantize_w(unit - 1)
+            quantize_w(last - 1)
 
-        X_AFTER = 4
-        for m in range(ROW_TILES):
-            if m == 0:
-                load_w(0, [0])
-                load_state(den_state, "den", 0)
-                load_w(0, [1])
-            elif m <= X_AFTER:
-                load_w(m, [0, 1])
-                load_state(den_state, "den", m)
-            else:
-                load_state(den_state, "den", m)
-                if m == ROW_TILES - 1:
-                    load_state(num_state, "num", 0)
-                load_w(m, [0, 1])
-            if m == X_AFTER:
-                load_x_scales()
-                load_x(0)
-            inverse_root(m)
-            if m < ROW_TILES - 1:
-                square(m)
-            if m == X_AFTER + 1:
-                square_on_vector(ROW_TILES)
-            if m == ROW_TILES - 1:
-                readout(0)
-            prepare_w(m)
+        def first_passes(g):
+            for step in range(AHEAD):
+                for block in range(2):
+                    project(step, block, g)
+
+        load_state(den_state, "den", 0, 0, HALF)
+        load_w(0, W_PIECES[0][0])
+        load_w(0, W_PIECES[0][1])
+        load_state(den_state, "den", 0, HALF, C)
+        prepare_w(0, 2)
+        inverse_root(0, 0, HALF)
+        square(0)
+        inverse_root(0, HALF, C)
+        square(1)
+        ready = 2
+        for g in range(PASSES):
+            for piece in W_PIECES[g]:
+                first, last = UNITS * g + piece[0], UNITS * g + piece[1]
+                if last <= ready:
+                    continue
+                if g == PASSES - 1:
+                    load_x_scales()
+                    load_x(X_PARTS[0])
+                    square_on_vector(11)
+                    for g0 in range(g):
+                        first_passes(g0)
+                load_w(g, piece)
+                prepare_w(first, last)
+                ready = last
+                for m in range(first // 2, last // 2):
+                    load_state(den_state, "den", m)
+                    inverse_root(m)
+                    if m == 1:
+                        square(2)
+                    elif m < 6:
+                        square(2 * m - 1)
+                        square(2 * m)
+        first_passes(PASSES - 1)
+        load_state(num_state, "num", 0)
         load_state(num_state, "num", 1)
-        load_state(num_state, "num", 2)
-        load_x(1)
-        for m in range(3, ROW_TILES):
+        load_x(X_PARTS[1])
+        for m in range(2, ROW_TILES):
             load_state(num_state, "num", m)
-        for step in range(3):
-            project(step)
+        readout(0)
+        readout(1)
 
-        to_square = [ROW_TILES - 1] + list(range(ROW_TILES + 1, STEPS))
-        for i in range(STEPS + 4):
+        to_square = list(range(12, STEPS))
+        on_vector = [1, 3, 5, 13, 14, 15]
+        for i in range(STEPS + 5):
             if i < STEPS:
                 receptance(i)
-            if i % 2 == 0 and 2 <= i < STEPS:
+            if 1 <= i <= STEPS and i - 1 not in on_vector:
                 round_y(i - 1, nc.scalar.copy)
             elif to_square:
                 square(to_square.pop(0))
             if 3 <= i < STEPS + 3:
                 gather_words(i - 3)
+            if 4 <= i < STEPS + 4:
+                store_planes(i - 4)
             if i < STEPS:
                 apply_gate(i)
-                store_y(i)
-            if i == 0:
-                quantize_w(2 * ROW_TILES - 1)
-            if i + 1 < STEPS:
-                readout(i + 1)
-            if 4 <= i:
-                quantize_y(i - 4)
-                store_planes(i - 4)
-            if i < STEPS and (i % 2 == 0 or i == STEPS - 1):
+                if i >= 12:
+                    store_y(i, i + 1)
+                elif i % 2 == 1:
+                    store_y(i - 1, i + 1)
+            if i + 2 < STEPS:
+                readout(i + 2)
+            if i in on_vector and i + 2 < STEPS:
                 round_y(i, nc.vector.tensor_copy)
-            if i + 3 < STEPS:
-                project(i + 3)
-            if 1 <= i < STEPS + 1:
+            if 3 <= i < STEPS + 3:
+                quantize_y(i - 3)
+            if i in on_vector and i + 2 >= STEPS:
+                round_y(i, nc.vector.tensor_copy)
+            if 1 <= i <= STEPS:
                 turn(i - 1)
+            if i + AHEAD < STEPS:
+                for block in range(2):
+                    for g in range(PASSES):
+                        project(i + AHEAD, block, g)

@@ -23,11 +23,9 @@ BANK = 512
 HALF = 1024
 ROW_TILES = M // P
 STEPS = 2 * ROW_TILES
-UNITS = C // BANK
-W_PIECES = [[(0, 1), (1, 2), (2, 4)], [(0, 2), (2, 4)], [(0, 4)], [(0, 4)]]
-X_PARTS = [(0, 2), (2, ROW_TILES)]
-WORD_PIECES = [(0, 2), (2, 4), (4, 6), (6, 7), (7, 8)]
-SCALE_PIECES = [(0, 7), (7, 8)]
+X_PARTS = [(0, 4), (4, ROW_TILES)]
+WORD_PIECES = [(0, 4), (4, 8), (8, 12), (12, 14), (14, 16)]
+SCALE_PIECES = [(0, 8), (8, 12), (12, 16)]
 AHEAD = 3
 
 
@@ -46,23 +44,22 @@ def tile_receptance_gated_state_readout_g6_kernel(
         ident = keep.tile([P, P], F32)
         make_identity(nc, ident[:])
 
-        w_rows, w_raw, w_grouped, w_codes, w_planes = {}, {}, {}, {}, {}
+        w_raw, w_grouped, w_codes, w_planes = {}, {}, {}, {}
         x_codes, state, work, z, gate = {}, {}, {}, {}, {}
         y_bf, turned, y_grouped, y_codes, y_planes = {}, {}, {}, {}, {}
 
-        def load_w(g, piece):
-            if g not in w_rows:
-                w_rows[g] = stream.tile([P, PACK * C], BF16, name="w_rows", bufs=2)
-            lo, hi = piece[0] * BANK, piece[1] * BANK
-            raw = w_rows[g][:, PACK * lo : PACK * hi].rearrange("p (j n) -> p j n", j=PACK)
-            rows = w_r[g * K_PASS : (g + 1) * K_PASS, lo:hi]
-            nc.sync.dma_start(out=raw, in_=rows.rearrange("(p j) n -> p j n", j=PACK))
-            for block in range(piece[0], piece[1]):
-                w_raw[UNITS * g + block] = raw[:, :, block * BANK - lo : (block + 1) * BANK - lo]
+        def load_w(slab, blocks):
+            half, g = divmod(slab, PASSES)
+            lo, hi = blocks[0] * BANK, (blocks[-1] + 1) * BANK
+            raw = stream.tile([P, PACK, hi - lo], BF16, name="w_raw", bufs=3)
+            rows = w_r[g * K_PASS : (g + 1) * K_PASS, half * HALF + lo : half * HALF + hi]
+            nc.sync.dma_start(out=raw[:], in_=rows.rearrange("(p j) n -> p j n", j=PACK))
+            for block in blocks:
+                w_raw[2 * slab + block] = raw[:, :, block * BANK - lo : (block + 1) * BANK - lo]
 
-        def interleave_w(unit):
+        def interleave_w(unit, copy):
             w_grouped[unit] = stream.tile([P, BANK * PACK], BF16, name="w_grouped", bufs=3, align_bytes=64)
-            nc.vector.tensor_copy(
+            copy(
                 out=w_grouped[unit][:].rearrange("p (c i j) -> p c j i", i=4, j=PACK),
                 in_=w_raw[unit].rearrange("p j (c i) -> p c j i", i=4),
             )
@@ -102,7 +99,7 @@ def tile_receptance_gated_state_readout_g6_kernel(
             nc.scalar.activation(out=work[m][:, lo:hi], in_=state["den", m][:, lo:hi], func=ACT.Abs_reciprocal_sqrt)
 
         def work_of(step):
-            m, half = divmod(step, 2)
+            half, m = divmod(step, ROW_TILES)
             return work[m][:, half * HALF : (half + 1) * HALF]
 
         def square(step):
@@ -112,15 +109,15 @@ def tile_receptance_gated_state_readout_g6_kernel(
             nc.vector.tensor_tensor(out=work_of(step), in0=work_of(step), in1=work_of(step), op=MULT)
 
         def readout(step):
-            m, half = divmod(step, 2)
+            half, m = divmod(step, ROW_TILES)
             num = state["num", m][:, half * HALF : (half + 1) * HALF]
             nc.vector.tensor_tensor(out=work_of(step), in0=work_of(step), in1=num, op=MULT)
 
         def project(step, block, g):
-            m, half = divmod(step, 2)
+            half, m = divmod(step, ROW_TILES)
             if g == 0:
                 z[step, block] = psum.tile([P, BANK], F32, name="z", bufs=2 * AHEAD)
-            unit = UNITS * g + 2 * half + block
+            unit = 2 * (PASSES * half + g) + block
             nc.tensor.matmul_mx(
                 out=z[step, block][:],
                 lhsT=x_codes[m][:, g, :].bitcast(FP8X4),
@@ -138,158 +135,192 @@ def tile_receptance_gated_state_readout_g6_kernel(
                     out=gate[step][:, block * BANK : (block + 1) * BANK], in_=z[step, block][:], func=ACT.Sigmoid
                 )
 
-        def apply_gate(step):
-            nc.vector.tensor_tensor(out=work_of(step), in0=work_of(step), in1=gate[step][:], op=MULT)
+        def apply_gate(step, lo, hi):
+            cols = slice(lo * BANK, hi * BANK)
+            nc.vector.tensor_tensor(
+                out=work_of(step)[:, cols], in0=work_of(step)[:, cols], in1=gate[step][:, cols], op=MULT
+            )
 
-        def round_y(step, copy):
-            y_bf[step] = stream.tile([P, HALF], BF16, name="y_bf", bufs=2)
+        def round_y(step, copy, lo, hi):
+            if lo == 0:
+                y_bf[step] = stream.tile([P, HALF], BF16, name="y_bf", bufs=2)
+            cols = slice(lo * BANK, hi * BANK)
             copy(
-                out=y_bf[step][:].rearrange("p (b u w e) -> p b u w e", b=2, u=2, e=2),
-                in_=work_of(step).rearrange("p (b w u e) -> p b u w e", b=2, u=2, e=2),
+                out=y_bf[step][:, cols].rearrange("p (b u w e) -> p b u w e", b=hi - lo, u=2, e=2),
+                in_=work_of(step)[:, cols].rearrange("p (b w u e) -> p b u w e", b=hi - lo, u=2, e=2),
             )
 
-        def turn(step):
-            turned[step] = psum.tile([P, 2, 2, P], F32, name="turned", bufs=2)
+        def turn(step, lo, hi):
+            turned[step, lo] = psum.tile([P, hi - lo, 2, P], F32, name="turned", bufs=2)
             words = y_bf[step][:].bitcast(F32)
-            for block in range(2):
+            for block in range(lo, hi):
                 for u in range(2):
-                    lo = (2 * block + u) * P
-                    nc.tensor.transpose(turned[step][:, block, u, :], words[:, lo : lo + P], ident[:])
+                    first = (2 * block + u) * P
+                    nc.tensor.transpose(turned[step, lo][:, block - lo, u, :], words[:, first : first + P], ident[:])
 
-        def gather_words(step):
-            y_grouped[step] = stream.tile([P, HALF], BF16, name="y_grouped", bufs=2, align_bytes=64)
+        def gather_words(step, lo, hi):
+            if lo == 0:
+                y_grouped[step] = stream.tile([P, HALF], BF16, name="y_grouped", bufs=2, align_bytes=64)
+            words = y_grouped[step][:, lo * BANK : hi * BANK].bitcast(F32)
             nc.scalar.copy(
-                out=y_grouped[step][:].bitcast(F32).rearrange("p (b m u) -> p b m u", b=2, u=2),
-                in_=turned[step][:].rearrange("p b u m -> p b m u"),
+                out=words.rearrange("p (b m u) -> p b m u", b=hi - lo, u=2),
+                in_=turned[step, lo][:].rearrange("p b u m -> p b m u"),
             )
 
-        def piece_of(pieces, m):
-            return [piece for piece in pieces if piece[0] <= m < piece[1]][0]
+        def piece_of(pieces, step):
+            return [piece for piece in pieces if piece[0] <= step < piece[1]][0]
 
-        def quantize_y(step):
-            m, half = divmod(step, 2)
-            words, scales = piece_of(WORD_PIECES, m), piece_of(SCALE_PIECES, m)
+        def quantize_y(step, lo, hi):
+            words, scales = piece_of(WORD_PIECES, step), piece_of(SCALE_PIECES, step)
             if words not in y_codes:
-                shape = [P, PASSES, (words[1] - words[0]) * P]
+                shape = [P, 2, (words[1] - words[0]) * P]
                 y_codes[words] = stream.tile(shape, U32, name="y_codes", bufs=3, align_bytes=64)
             if scales not in y_planes:
-                shape = [P, PASSES, (scales[1] - scales[0]) * P]
+                shape = [P, 2, (scales[1] - scales[0]) * P]
                 y_planes[scales] = keep.tile(shape, U8, name="y_plane%d" % scales[0], align_bytes=64)
-            for block in range(2):
-                g = 2 * half + block
-                lo, lo_s = (m - words[0]) * P, (m - scales[0]) * P
+            at_word, at_scale = (step - words[0]) * P, (step - scales[0]) * P
+            for block in range(lo, hi):
                 nc.vector.quantize_mx(
-                    out=y_codes[words][:, g, lo : lo + P].bitcast(FP8X4),
-                    scales=y_planes[scales][:, g, lo_s : lo_s + P],
+                    out=y_codes[words][:, block, at_word : at_word + P].bitcast(FP8X4),
+                    scales=y_planes[scales][:, block, at_scale : at_scale + P],
                     in_=y_grouped[step][:, block * BANK : (block + 1) * BANK],
                 )
 
-        def store_y(first, last):
-            m, half = divmod(first, 2)
-            lo, hi = half * HALF, (half + last - first) * HALF
-            nc.sync.dma_start(out=out_0[m * P : (m + 1) * P, lo:hi], in_=work[m][:, lo:hi])
+        def store_y(step):
+            half, m = divmod(step, ROW_TILES)
+            nc.sync.dma_start(out=out_0[m * P : (m + 1) * P, half * HALF : (half + 1) * HALF], in_=work_of(step))
 
         def store_planes(step):
-            m, half = divmod(step, 2)
-            words, scales = piece_of(WORD_PIECES, m), piece_of(SCALE_PIECES, m)
-            if half == 1 and m + 1 == words[1]:
-                merged = out_1.rearrange("g p m t -> p g (m t)")
+            half, m = divmod(step, ROW_TILES)
+            words, scales = piece_of(WORD_PIECES, step), piece_of(SCALE_PIECES, step)
+            groups = slice(2 * half, 2 * half + 2)
+            if step + 1 == words[1]:
+                merged = out_1[groups].rearrange("g p m t -> p g (m t)")
+                first = words[0] % ROW_TILES
                 nc.sync.dma_start(
-                    out=merged[:, :, words[0] * P * PACK : words[1] * P * PACK].bitcast(I32),
+                    out=merged[:, :, first * P * PACK : (m + 1) * P * PACK].bitcast(I32),
                     in_=y_codes[words][:].bitcast(I32),
                 )
-            if half == 1 and m + 1 == scales[1]:
+            if step + 1 == scales[1]:
+                first = scales[0] % ROW_TILES
                 for quad in range(4):
-                    rows = out_2[:, 4 * quad : 4 * quad + 4, scales[0] * P : scales[1] * P]
+                    rows = out_2[groups, 4 * quad : 4 * quad + 4, first * P : (m + 1) * P]
                     queue = nc.scalar if step == STEPS - 1 and quad >= 2 else nc.sync
                     queue.dma_start(
                         out=rows.rearrange("g r m -> r g m").bitcast(I32),
                         in_=y_planes[scales][32 * quad : 32 * quad + 4, :, :].bitcast(I32),
                     )
 
-        def prepare_w(first, last):
-            for unit in range(first, last):
-                interleave_w(unit)
-                if unit > first:
-                    quantize_w(unit - 1)
-            quantize_w(last - 1)
+        def prepare_w(slab):
+            interleave_w(2 * slab, nc.vector.tensor_copy)
+            interleave_w(2 * slab + 1, nc.vector.tensor_copy)
+            quantize_w(2 * slab)
+            quantize_w(2 * slab + 1)
 
-        def first_passes(g):
-            for step in range(AHEAD):
-                for block in range(2):
+        def project_step(step):
+            for block in range(2):
+                for g in range(PASSES):
                     project(step, block, g)
 
+        def next_den(m):
+            load_state(den_state, "den", m)
+            inverse_root(m)
+
         load_state(den_state, "den", 0, 0, HALF)
-        load_w(0, W_PIECES[0][0])
-        load_w(0, W_PIECES[0][1])
+        load_w(0, [0])
+        load_w(0, [1])
         load_state(den_state, "den", 0, HALF, C)
-        prepare_w(0, 2)
+        prepare_w(0)
         inverse_root(0, 0, HALF)
         square(0)
         inverse_root(0, HALF, C)
+        square_on_vector(8)
+        next_den(1)
         square(1)
-        ready = 2
-        for g in range(PASSES):
-            for piece in W_PIECES[g]:
-                first, last = UNITS * g + piece[0], UNITS * g + piece[1]
-                if last <= ready:
-                    continue
-                if g == PASSES - 1:
-                    load_x_scales()
-                    load_x(X_PARTS[0])
-                    square_on_vector(11)
-                    for g0 in range(g):
-                        first_passes(g0)
-                load_w(g, piece)
-                prepare_w(first, last)
-                ready = last
-                for m in range(first // 2, last // 2):
-                    load_state(den_state, "den", m)
-                    inverse_root(m)
-                    if m == 1:
-                        square(2)
-                    elif m < 6:
-                        square(2 * m - 1)
-                        square(2 * m)
-        first_passes(PASSES - 1)
+        for slab in range(1, PASSES):
+            load_w(slab, [0, 1])
+            prepare_w(slab)
+            next_den(slab + 1)
+            if slab + 1 < 4:
+                square(slab + 1)
+        next_den(5)
+        load_x_scales()
+        load_x(X_PARTS[0])
+        for step in range(AHEAD):
+            project_step(step)
+        for step in range(9, 13):
+            square_on_vector(step)
+        next_den(6)
+        square(4)
+        load_w(4, [0, 1])
+        prepare_w(4)
+        next_den(7)
         load_state(num_state, "num", 0)
         load_state(num_state, "num", 1)
+        load_w(5, [0, 1])
+        load_state(num_state, "num", 2)
+        load_w(6, [0, 1])
+        load_state(num_state, "num", 3)
         load_x(X_PARTS[1])
-        for m in range(2, ROW_TILES):
+        load_w(7, [0, 1])
+        for m in range(4, ROW_TILES):
             load_state(num_state, "num", m)
         readout(0)
         readout(1)
 
-        to_square = list(range(12, STEPS))
-        on_vector = [1, 3, 5, 13, 14, 15]
-        for i in range(STEPS + 5):
+        scalar_squares = {0: 5, 1: 6, 2: 7, 7: 13, 9: 14, 11: 15}
+        scalar_units = {1: 11, 3: 13, 4: 14, 5: 15}
+        vector_units = {0: 10, 1: 12}
+        scalar_rounds = [5, 7, 9, 11, 12]
+        last = STEPS - 1
+        laid = []
+        for i in range(STEPS + 4):
+            to_quantize, laid = laid, []
             if i < STEPS:
                 receptance(i)
-            if 1 <= i <= STEPS and i - 1 not in on_vector:
-                round_y(i - 1, nc.scalar.copy)
-            elif to_square:
-                square(to_square.pop(0))
-            if 3 <= i < STEPS + 3:
-                gather_words(i - 3)
-            if 4 <= i < STEPS + 4:
+            if i in scalar_squares:
+                square(scalar_squares[i])
+            if i in scalar_units:
+                interleave_w(scalar_units[i], nc.scalar.copy)
+                laid.append(scalar_units[i])
+            if i - 1 in scalar_rounds:
+                round_y(i - 1, nc.scalar.copy, 0, 2)
+            if 0 <= i - 3 < last:
+                gather_words(i - 3, 0, 2)
+            if 0 <= i - 4:
                 store_planes(i - 4)
+            if i < last:
+                apply_gate(i, 0, 2)
+            if i == last:
+                apply_gate(i, 0, 1)
+                apply_gate(i, 1, 2)
             if i < STEPS:
-                apply_gate(i)
-                if i >= 12:
-                    store_y(i, i + 1)
-                elif i % 2 == 1:
-                    store_y(i - 1, i + 1)
+                store_y(i)
+            for unit in to_quantize:
+                quantize_w(unit)
+            if i in vector_units:
+                interleave_w(vector_units[i], nc.vector.tensor_copy)
+                laid.append(vector_units[i])
             if i + 2 < STEPS:
                 readout(i + 2)
-            if i in on_vector and i + 2 < STEPS:
-                round_y(i, nc.vector.tensor_copy)
-            if 3 <= i < STEPS + 3:
-                quantize_y(i - 3)
-            if i in on_vector and i + 2 >= STEPS:
-                round_y(i, nc.vector.tensor_copy)
-            if 1 <= i <= STEPS:
-                turn(i - 1)
-            if i + AHEAD < STEPS:
+                if i not in scalar_rounds:
+                    round_y(i, nc.vector.tensor_copy, 0, 2)
+            if i == last:
+                round_y(i, nc.vector.tensor_copy, 0, 1)
+                round_y(i, nc.vector.tensor_copy, 1, 2)
+            if 0 <= i - 3 < last:
+                quantize_y(i - 3, 0, 2)
+            if i == last - 1:
+                round_y(i, nc.vector.tensor_copy, 0, 2)
+            if AHEAD <= i + 2 < STEPS:
+                project_step(i + 2)
+            if 0 <= i - 1 < last:
+                turn(i - 1, 0, 2)
+            if i - 1 == last:
+                turn(last, 0, 1)
+            if i - 2 == last:
+                turn(last, 1, 2)
+            if i - 3 == last:
                 for block in range(2):
-                    for g in range(PASSES):
-                        project(i + AHEAD, block, g)
+                    gather_words(last, block, block + 1)
+                    quantize_y(last, block, block + 1)

@@ -23,8 +23,8 @@ BANK = 512
 HALF = 1024
 ROW_TILES = M // P
 STEPS = 2 * ROW_TILES
-X_PARTS = [(0, 4), (4, ROW_TILES)]
-WORD_PIECES = [(0, 4), (4, 8), (8, 12), (12, 14), (14, 16)]
+X_PARTS = [(0, 3), (3, ROW_TILES)]
+WORD_PIECES = [(0, 4), (4, 8), (8, 10), (10, 12), (12, 14), (14, 15), (15, 16)]
 SCALE_PIECES = [(0, 8), (8, 12), (12, 16)]
 AHEAD = 3
 
@@ -174,7 +174,7 @@ def tile_receptance_gated_state_readout_g6_kernel(
             words, scales = piece_of(WORD_PIECES, step), piece_of(SCALE_PIECES, step)
             if words not in y_codes:
                 shape = [P, 2, (words[1] - words[0]) * P]
-                y_codes[words] = stream.tile(shape, U32, name="y_codes", bufs=3, align_bytes=64)
+                y_codes[words] = stream.tile(shape, U32, name="y_codes", bufs=4, align_bytes=64)
             if scales not in y_planes:
                 shape = [P, 2, (scales[1] - scales[0]) * P]
                 y_planes[scales] = keep.tile(shape, U8, name="y_plane%d" % scales[0], align_bytes=64)
@@ -244,34 +244,37 @@ def tile_receptance_gated_state_readout_g6_kernel(
             if slab + 1 < 4:
                 square(slab + 1)
         next_den(5)
+        next_den(6)
+        square(4)
         load_x_scales()
         load_x(X_PARTS[0])
         for step in range(AHEAD):
             project_step(step)
-        for step in range(9, 13):
+        for step in range(9, 14):
             square_on_vector(step)
-        next_den(6)
-        square(4)
+        next_den(7)
+        load_state(num_state, "num", 0, 0, HALF)
+        readout(0)
         load_w(4, [0, 1])
         prepare_w(4)
-        next_den(7)
-        load_state(num_state, "num", 0)
-        load_state(num_state, "num", 1)
-        load_w(5, [0, 1])
-        load_state(num_state, "num", 2)
-        load_w(6, [0, 1])
-        load_state(num_state, "num", 3)
-        load_x(X_PARTS[1])
-        load_w(7, [0, 1])
-        for m in range(4, ROW_TILES):
-            load_state(num_state, "num", m)
-        readout(0)
+        load_state(num_state, "num", 1, 0, HALF)
         readout(1)
+        load_w(5, [0, 1])
+        load_state(num_state, "num", 2, 0, HALF)
+        load_x(X_PARTS[1])
+        load_state(num_state, "num", 3, 0, HALF)
+        load_w(6, [0, 1])
+        load_state(num_state, "num", 4, 0, HALF)
+        load_w(7, [0, 1])
+        for m in range(5, ROW_TILES):
+            load_state(num_state, "num", m, 0, HALF)
+        for m in range(ROW_TILES):
+            load_state(num_state, "num", m, HALF, C)
 
-        scalar_squares = {0: 5, 1: 6, 2: 7, 7: 13, 9: 14, 11: 15}
+        scalar_squares = {0: 5, 1: 6, 2: 7, 7: 14, 9: 15}
         scalar_units = {1: 11, 3: 13, 4: 14, 5: 15}
         vector_units = {0: 10, 1: 12}
-        scalar_rounds = [5, 7, 9, 11, 12]
+        scalar_rounds = [5, 7, 9, 10, 11, 12]
         last = STEPS - 1
         laid = []
         for i in range(STEPS + 4):
@@ -310,6 +313,8 @@ def tile_receptance_gated_state_readout_g6_kernel(
                 round_y(i, nc.vector.tensor_copy, 1, 2)
             if 0 <= i - 3 < last:
                 quantize_y(i - 3, 0, 2)
+            if i == 5:
+                quantize_w(laid.pop())
             if i == last - 1:
                 round_y(i, nc.vector.tensor_copy, 0, 2)
             if AHEAD <= i + 2 < STEPS:

from contextlib import ExitStack

import concourse.mybir as mybir
from concourse.masks import make_identity

M, C = 1024, 2048
FLOPS = 2 * M * C * C

F32 = mybir.dt.float32
BF16 = mybir.dt.bfloat16
I32 = mybir.dt.int32
U32 = mybir.dt.uint32
U8 = mybir.dt.uint8
FP8X4 = mybir.dt.float8_e4m3fn_x4
ACT = mybir.ActivationFunctionType
MULT = mybir.AluOpType.mult

P = 128
PACK = 4
K_PASS = P * PACK
PASSES = C // K_PASS
BANK = 512
HALF = 1024
ROW_TILES = M // P
STEPS = 2 * ROW_TILES
X_PARTS = [(0, 3), (3, ROW_TILES)]
WORD_PIECES = [(0, 4), (4, 8), (8, 10), (10, 12), (12, 14), (14, 15), (15, 16)]
SCALE_PIECES = [(0, 8), (8, 12), (12, 16)]
AHEAD = 3


def tile_receptance_gated_state_readout_g6_kernel(
    tc, x_words, x_scales, w_r, num_state, den_state, out_0, out_1, out_2
):
    nc = tc.nc
    with ExitStack() as ctx:
        keep = ctx.enter_context(tc.tile_pool(name="keep", bufs=1))
        stream = ctx.enter_context(tc.tile_pool(name="stream", bufs=3))
        psum = ctx.enter_context(tc.psum_pool(name="psum", bufs=2))
        ctx.enter_context(tc.manual_schedule())

        x_plane = keep.tile([P, M], U8, align_bytes=64)
        nc.gpsimd.memset(x_plane[:].bitcast(I32), 0)
        ident = keep.tile([P, P], F32)
        make_identity(nc, ident[:])

        w_raw, w_grouped, w_codes, w_planes = {}, {}, {}, {}
        x_codes, state, work, z, gate = {}, {}, {}, {}, {}
        y_bf, turned, y_grouped, y_codes, y_planes = {}, {}, {}, {}, {}

        def load_w(slab, blocks):
            half, g = divmod(slab, PASSES)
            lo, hi = blocks[0] * BANK, (blocks[-1] + 1) * BANK
            raw = stream.tile([P, PACK, hi - lo], BF16, name="w_raw", bufs=3)
            rows = w_r[g * K_PASS : (g + 1) * K_PASS, half * HALF + lo : half * HALF + hi]
            nc.sync.dma_start(out=raw[:], in_=rows.rearrange("(p j) n -> p j n", j=PACK))
            for block in blocks:
                w_raw[2 * slab + block] = raw[:, :, block * BANK - lo : (block + 1) * BANK - lo]

        def interleave_w(unit, copy):
            w_grouped[unit] = stream.tile([P, BANK * PACK], BF16, name="w_grouped", bufs=3, align_bytes=64)
            copy(
                out=w_grouped[unit][:].rearrange("p (c i j) -> p c j i", i=4, j=PACK),
                in_=w_raw[unit].rearrange("p j (c i) -> p c j i", i=4),
            )

        def quantize_w(unit):
            w_codes[unit] = keep.tile([P, BANK], U32, name="w_codes%d" % unit, align_bytes=64)
            w_planes[unit] = keep.tile([P, BANK], U8, name="w_plane%d" % unit, align_bytes=64)
            nc.vector.quantize_mx(
                out=w_codes[unit][:].bitcast(FP8X4), scales=w_planes[unit][:], in_=w_grouped[unit][:]
            )

        def load_state(src, key, m, lo=0, hi=C):
            if (key, m) not in state:
                state[key, m] = stream.tile([P, C], BF16, name="state", bufs=ROW_TILES)
            nc.sync.dma_start(out=state[key, m][:, lo:hi], in_=src[m * P : (m + 1) * P, lo:hi])

        def load_x_scales():
            for quad in range(4):
                nc.sync.dma_start(
                    out=x_plane[32 * quad : 32 * quad + 16, :].bitcast(I32),
                    in_=x_scales[:, 4 * quad : 4 * quad + 4, :].bitcast(I32),
                )

        def load_x(part):
            first, last = part
            codes = keep.tile([P, PASSES, (last - first) * P], U32, name="x_codes%d" % first, align_bytes=64)
            merged = x_words.rearrange("g p n t -> p g (n t)")
            nc.sync.dma_start(
                out=codes[:].bitcast(I32), in_=merged[:, :, first * P * PACK : last * P * PACK].bitcast(I32)
            )
            for m in range(first, last):
                x_codes[m] = codes[:, :, (m - first) * P : (m - first + 1) * P]

        def inverse_root(m, lo=0, hi=C):
            if m not in work:
                work[m] = keep.tile([P, C], F32, name="work%d" % m)
            nc.scalar.activation(out=work[m][:, lo:hi], in_=state["den", m][:, lo:hi], func=ACT.Abs_reciprocal_sqrt)

        def work_of(step):
            half, m = divmod(step, ROW_TILES)
            return work[m][:, half * HALF : (half + 1) * HALF]

        def square(step):
            nc.scalar.activation(out=work_of(step), in_=work_of(step), func=ACT.Square)

        def square_on_vector(step):
            nc.vector.tensor_tensor(out=work_of(step), in0=work_of(step), in1=work_of(step), op=MULT)

        def readout(step):
            half, m = divmod(step, ROW_TILES)
            num = state["num", m][:, half * HALF : (half + 1) * HALF]
            nc.vector.tensor_tensor(out=work_of(step), in0=work_of(step), in1=num, op=MULT)

        def project(step, block, g):
            half, m = divmod(step, ROW_TILES)
            if g == 0:
                z[step, block] = psum.tile([P, BANK], F32, name="z", bufs=2 * AHEAD)
            unit = 2 * (PASSES * half + g) + block
            nc.tensor.matmul_mx(
                out=z[step, block][:],
                lhsT=x_codes[m][:, g, :].bitcast(FP8X4),
                lhsT_scale=x_plane[4 * g :, m * P : (m + 1) * P],
                rhs=w_codes[unit][:].bitcast(FP8X4),
                rhs_scale=w_planes[unit][:],
                start=(g == 0),
                stop=(g == PASSES - 1),
            )

        def receptance(step):
            gate[step] = stream.tile([P, HALF], F32, name="gate", bufs=3)
            for block in range(2):
                nc.scalar.activation(
                    out=gate[step][:, block * BANK : (block + 1) * BANK], in_=z[step, block][:], func=ACT.Sigmoid
                )

        def apply_gate(step, lo, hi):
            cols = slice(lo * BANK, hi * BANK)
            nc.vector.tensor_tensor(
                out=work_of(step)[:, cols], in0=work_of(step)[:, cols], in1=gate[step][:, cols], op=MULT
            )

        def round_y(step, copy, lo, hi):
            if lo == 0:
                y_bf[step] = stream.tile([P, HALF], BF16, name="y_bf", bufs=2)
            cols = slice(lo * BANK, hi * BANK)
            copy(
                out=y_bf[step][:, cols].rearrange("p (b u w e) -> p b u w e", b=hi - lo, u=2, e=2),
                in_=work_of(step)[:, cols].rearrange("p (b w u e) -> p b u w e", b=hi - lo, u=2, e=2),
            )

        def turn(step, lo, hi):
            turned[step, lo] = psum.tile([P, hi - lo, 2, P], F32, name="turned", bufs=2)
            words = y_bf[step][:].bitcast(F32)
            for block in range(lo, hi):
                for u in range(2):
                    first = (2 * block + u) * P
                    nc.tensor.transpose(turned[step, lo][:, block - lo, u, :], words[:, first : first + P], ident[:])

        def gather_words(step, lo, hi):
            if lo == 0:
                y_grouped[step] = stream.tile([P, HALF], BF16, name="y_grouped", bufs=2, align_bytes=64)
            words = y_grouped[step][:, lo * BANK : hi * BANK].bitcast(F32)
            nc.scalar.copy(
                out=words.rearrange("p (b m u) -> p b m u", b=hi - lo, u=2),
                in_=turned[step, lo][:].rearrange("p b u m -> p b m u"),
            )

        def piece_of(pieces, step):
            return [piece for piece in pieces if piece[0] <= step < piece[1]][0]

        def quantize_y(step, lo, hi):
            words, scales = piece_of(WORD_PIECES, step), piece_of(SCALE_PIECES, step)
            if words not in y_codes:
                shape = [P, 2, (words[1] - words[0]) * P]
                y_codes[words] = stream.tile(shape, U32, name="y_codes", bufs=4, align_bytes=64)
            if scales not in y_planes:
                shape = [P, 2, (scales[1] - scales[0]) * P]
                y_planes[scales] = keep.tile(shape, U8, name="y_plane%d" % scales[0], align_bytes=64)
            at_word, at_scale = (step - words[0]) * P, (step - scales[0]) * P
            for block in range(lo, hi):
                nc.vector.quantize_mx(
                    out=y_codes[words][:, block, at_word : at_word + P].bitcast(FP8X4),
                    scales=y_planes[scales][:, block, at_scale : at_scale + P],
                    in_=y_grouped[step][:, block * BANK : (block + 1) * BANK],
                )

        def store_y(step):
            half, m = divmod(step, ROW_TILES)
            nc.sync.dma_start(out=out_0[m * P : (m + 1) * P, half * HALF : (half + 1) * HALF], in_=work_of(step))

        def store_planes(step):
            half, m = divmod(step, ROW_TILES)
            words, scales = piece_of(WORD_PIECES, step), piece_of(SCALE_PIECES, step)
            groups = slice(2 * half, 2 * half + 2)
            if step + 1 == words[1]:
                merged = out_1[groups].rearrange("g p m t -> p g (m t)")
                first = words[0] % ROW_TILES
                nc.sync.dma_start(
                    out=merged[:, :, first * P * PACK : (m + 1) * P * PACK].bitcast(I32),
                    in_=y_codes[words][:].bitcast(I32),
                )
            if step + 1 == scales[1]:
                first = scales[0] % ROW_TILES
                for quad in range(4):
                    rows = out_2[groups, 4 * quad : 4 * quad + 4, first * P : (m + 1) * P]
                    queue = nc.scalar if step == STEPS - 1 and quad >= 2 else nc.sync
                    queue.dma_start(
                        out=rows.rearrange("g r m -> r g m").bitcast(I32),
                        in_=y_planes[scales][32 * quad : 32 * quad + 4, :, :].bitcast(I32),
                    )

        def prepare_w(slab):
            interleave_w(2 * slab, nc.vector.tensor_copy)
            interleave_w(2 * slab + 1, nc.vector.tensor_copy)
            quantize_w(2 * slab)
            quantize_w(2 * slab + 1)

        def project_step(step):
            for block in range(2):
                for g in range(PASSES):
                    project(step, block, g)

        def next_den(m):
            load_state(den_state, "den", m)
            inverse_root(m)

        load_state(den_state, "den", 0, 0, HALF)
        load_w(0, [0])
        load_w(0, [1])
        load_state(den_state, "den", 0, HALF, C)
        prepare_w(0)
        inverse_root(0, 0, HALF)
        square(0)
        inverse_root(0, HALF, C)
        square_on_vector(8)
        next_den(1)
        square(1)
        for slab in range(1, PASSES):
            load_w(slab, [0, 1])
            prepare_w(slab)
            next_den(slab + 1)
            if slab + 1 < 4:
                square(slab + 1)
        next_den(5)
        next_den(6)
        square(4)
        load_x_scales()
        load_x(X_PARTS[0])
        for step in range(AHEAD):
            project_step(step)
        for step in range(9, 14):
            square_on_vector(step)
        next_den(7)
        load_state(num_state, "num", 0, 0, HALF)
        readout(0)
        load_w(4, [0, 1])
        prepare_w(4)
        load_state(num_state, "num", 1, 0, HALF)
        readout(1)
        load_w(5, [0, 1])
        load_state(num_state, "num", 2, 0, HALF)
        load_x(X_PARTS[1])
        load_state(num_state, "num", 3, 0, HALF)
        load_w(6, [0, 1])
        load_state(num_state, "num", 4, 0, HALF)
        load_w(7, [0, 1])
        for m in range(5, ROW_TILES):
            load_state(num_state, "num", m, 0, HALF)
        for m in range(ROW_TILES):
            load_state(num_state, "num", m, HALF, C)

        scalar_squares = {0: 5, 1: 6, 2: 7, 7: 14, 9: 15}
        scalar_units = {1: 11, 3: 13, 4: 14, 5: 15}
        vector_units = {0: 10, 1: 12}
        scalar_rounds = [5, 7, 9, 10, 11, 12]
        last = STEPS - 1
        laid = []
        for i in range(STEPS + 4):
            to_quantize, laid = laid, []
            if i < STEPS:
                receptance(i)
            if i in scalar_squares:
                square(scalar_squares[i])
            if i in scalar_units:
                interleave_w(scalar_units[i], nc.scalar.copy)
                laid.append(scalar_units[i])
            if i - 1 in scalar_rounds:
                round_y(i - 1, nc.scalar.copy, 0, 2)
            if 0 <= i - 3 < last:
                gather_words(i - 3, 0, 2)
            if 0 <= i - 4:
                store_planes(i - 4)
            if i < last:
                apply_gate(i, 0, 2)
            if i == last:
                apply_gate(i, 0, 1)
                apply_gate(i, 1, 2)
            if i < STEPS:
                store_y(i)
            for unit in to_quantize:
                quantize_w(unit)
            if i in vector_units:
                interleave_w(vector_units[i], nc.vector.tensor_copy)
                laid.append(vector_units[i])
            if i + 2 < STEPS:
                readout(i + 2)
                if i not in scalar_rounds:
                    round_y(i, nc.vector.tensor_copy, 0, 2)
            if i == last:
                round_y(i, nc.vector.tensor_copy, 0, 1)
                round_y(i, nc.vector.tensor_copy, 1, 2)
            if 0 <= i - 3 < last:
                quantize_y(i - 3, 0, 2)
            if i == 5:
                quantize_w(laid.pop())
            if i == last - 1:
                round_y(i, nc.vector.tensor_copy, 0, 2)
            if AHEAD <= i + 2 < STEPS:
                project_step(i + 2)
            if 0 <= i - 1 < last:
                turn(i - 1, 0, 2)
            if i - 1 == last:
                turn(last, 0, 1)
            if i - 2 == last:
                turn(last, 1, 2)
            if i - 3 == last:
                for block in range(2):
                    gather_words(last, block, block + 1)
                    quantize_y(last, block, block + 1)
